import numpy as np
import ml_dtypes


def mxq(x, axis, fmt="e4m3"):
    dtype, down = {"e4m3": (ml_dtypes.float8_e4m3fn, 7), "e5m2": (ml_dtypes.float8_e5m2, 14)}[fmt]
    v = np.moveaxis(np.asarray(x, np.float32).astype(ml_dtypes.bfloat16).astype(np.float64), axis, -1)
    blocks = v.reshape(v.shape[:-1] + (-1, 32))
    amax = np.abs(blocks).max(-1, keepdims=True)
    byte = np.maximum(np.where(amax > 0, np.frexp(amax)[1] - 1 + 127, 0) - down, 1)
    scale = np.exp2(byte - 127.0)
    codes = (blocks / scale).astype(np.float32).astype(dtype).astype(np.float64)
    return np.moveaxis((codes * scale).reshape(v.shape), -1, axis)


WIDE = False


def mx_kscale(k):
    if not WIDE:
        return np.ones(k)
    levels = np.array([30, -30])
    if k % 512:
        return np.exp2(np.random.permutation(np.resize(levels, k // 32))).repeat(32)
    a = np.empty((k // 512, 16))
    for p in range(k // 512):
        a[p, :8] = np.random.permutation(np.resize(levels, 8))
        for g in range(8):
            far = levels[np.abs(levels - a[p, g]) >= 10]
            a[p, g + 8] = far[np.random.randint(len(far))]
    return np.exp2(a.ravel()).repeat(32)


def f64(x):
    return np.asarray(x).astype(np.float64)


E2M1 = np.array([0.0, 0.5, 1.0, 1.5, 2.0, 3.0, 4.0, 6.0, -0.0, -0.5, -1.0, -1.5, -2.0, -3.0, -4.0, -6.0])


def pack_weight(w, fmt):
    k, n = w.shape
    w = f64(np.asarray(w, np.float32).astype(ml_dtypes.bfloat16)).reshape(k // 32, 32, n)
    amax = np.abs(w).max(1)
    if fmt == "e4m3":
        byte = np.frexp(amax)[1] - 1 + 127 - 7
    else:
        mant, ex = np.frexp(amax / 6.0)
        byte = np.where(mant > 0.5, ex, ex - 1) + 127
    byte = np.clip(np.where(amax > 0, byte, 1), 1, 254)
    scaled = (w * np.exp2(127.0 - byte)[:, None, :]).reshape(k, n).astype(np.float32)
    by_word = np.ascontiguousarray(scaled.reshape(k // 512, 128, 4, n).transpose(0, 1, 3, 2))
    if fmt == "e4m3":
        words = by_word.astype(ml_dtypes.float8_e4m3fn).view(np.uint8)
    else:
        c = by_word.astype(ml_dtypes.float4_e2m1fn).view(np.uint8) & 0xF
        words = (c[..., 0::2] | (c[..., 1::2] << 4)).reshape(k // 512, 128, 2 * n)
    return np.ascontiguousarray(words), np.ascontiguousarray(byte.astype(np.uint8).reshape(k // 512, 16, n))


def unpack_weight(words, scales, fmt):
    g, _, n = scales.shape
    words = np.ascontiguousarray(words).reshape(g, 128, n, -1)
    if fmt == "e4m3":
        vals = words.view(ml_dtypes.float8_e4m3fn).astype(np.float64)
    else:
        nib = np.empty((g, 128, n, 4), np.uint8)
        nib[..., 0::2] = words & 0xF
        nib[..., 1::2] = words >> 4
        vals = E2M1[nib]
    vals = vals * np.repeat(np.exp2(scales.astype(np.float64) - 127.0), 8, axis=1)[..., None]
    return vals.transpose(0, 1, 3, 2).reshape(g * 512, n)


K, T, N = 1024, 512, 512


def setup_inputs():
    n = np.random.standard_normal
    fk = mx_kscale(K)
    wap = pack_weight(n((K, N)) * 1 / np.sqrt(K) * fk[:, None], "e2m1")
    wbp = pack_weight(n((K, N)) * 1 / np.sqrt(K) * fk[:, None], "e4m3")
    wcp = pack_weight(n((K, N)) * 1 / np.sqrt(K) * fk[:, None], "e2m1")
    return {
        "xf": (n((K, T))).astype(np.float32),
        "fa": (np.random.uniform(0.5, 2.0, (K, 1)) / fk[:, None]).astype(np.float32),
        "fb": (np.random.uniform(0.5, 2.0, (K, 1)) / fk[:, None]).astype(np.float32),
        "fd": (np.random.uniform(0.5, 2.0, (K, 1)) / fk[:, None]).astype(np.float32),
        "wa_words": wap[0],
        "wa_scales": wap[1],
        "wb_words": wbp[0],
        "wb_scales": wbp[1],
        "wc_words": wcp[0],
        "wc_scales": wcp[1],
    }


def reference(xf, fa, fb, fd, wa_words, wa_scales, wb_words, wb_scales, wc_words, wc_scales):
    wau = unpack_weight(wa_words, wa_scales, "e2m1")
    wbu = unpack_weight(wb_words, wb_scales, "e4m3")
    wcu = unpack_weight(wc_words, wc_scales, "e2m1")
    ua = f64(xf) * f64(fa)
    x1 = np.pad(f64(xf), ((0, 0), (1, 0)))[:, :T]
    ub = x1 * f64(fb)
    x2 = np.pad(f64(xf), ((0, 0), (2, 0)))[:, :T]
    uc = x2 * f64(fd)
    uaq = mxq(ua, 0, "e4m3")
    ubq = mxq(ub, 0, "e5m2")
    ucq = mxq(uc, 0, "e4m3")
    z = wau.T @ uaq + wbu.T @ ubq + wcu.T @ ucq
    y = np.maximum(z, 0.0)
    return y

@@ -1,0 +1,194 @@
+from contextlib import ExitStack
+
+import concourse.mybir as mybir
+
+K, T, N = 1024, 512, 512
+FLOPS = 3 * 2 * K * T * N
+
+F32 = mybir.dt.float32
+BF16 = mybir.dt.bfloat16
+I32 = mybir.dt.int32
+U32 = mybir.dt.uint32
+U8 = mybir.dt.uint8
+E4M3 = mybir.dt.float8_e4m3fn_x4
+E5M2 = mybir.dt.float8_e5m2_x4
+E2M1 = mybir.dt.float4_e2m1fn_x4
+ALU = mybir.AluOpType
+ACT = mybir.ActivationFunctionType
+
+P = 128
+PACK = 4
+PASSES = K // (P * PACK)
+M_TILES = N // P
+X0_CHUNKS = ((0, 128), (128, 256), (256, 512))
+
+
+def tile_mix_three_windows_one_sum_kernel(
+    tc, xf, fa, fb, fd, wa_words, wa_scales, wb_words, wb_scales, wc_words, wc_scales, out
+):
+    nc = tc.nc
+    with ExitStack() as ctx:
+        sb = ctx.enter_context(tc.tile_pool(name="sb", bufs=1))
+        ps = ctx.enter_context(tc.psum_pool(name="ps", bufs=1))
+        ctx.enter_context(tc.manual_schedule())
+
+        x_rows = xf.rearrange("(g p j) t -> g p j t", g=PASSES, j=PACK)
+
+        def load_x(g, t0, t1):
+            xt = sb.tile([P, PACK, t1 - t0], F32, name="x_%d_%d" % (g, t0), align_bytes=64)
+            nc.sync.dma_start(out=xt[:], in_=x_rows[g, :, :, t0:t1])
+            return xt
+
+        def load_factor(name, f):
+            ft = sb.tile([P, PASSES, 8], F32, name=name)
+            nc.sync.dma_start(out=ft[:, :, 0:PACK], in_=f.rearrange("(g p j) o -> p g (j o)", g=PASSES, j=PACK))
+            return ft
+
+        def load_words(name, words):
+            wt = sb.tile([P, PASSES, words.shape[2]], U8, name=name, align_bytes=64)
+            nc.sync.dma_start(out=wt[:].bitcast(I32), in_=words.rearrange("g p b -> p g b").bitcast(I32))
+            return wt
+
+        def new_plane(name):
+            plane = sb.tile([P, PASSES, N], U8, name=name, align_bytes=64)
+            nc.vector.memset(plane[:].bitcast(I32), 0)
+            return plane
+
+        def load_plane(queue, plane, scales):
+            rows = scales.rearrange("g (q r) n -> r q g n", r=4)
+            for r in range(4):
+                queue.dma_start(out=plane[r:P:32].bitcast(I32), in_=rows[r].bitcast(I32))
+
+        def new_u(name, width, pad):
+            u = sb.tile([P, PACK * width], BF16, name=name, align_bytes=64)
+            if pad:
+                nc.vector.memset(u[:, 0 : PACK * pad], 0.0)
+            return u
+
+        def scale_on_vector(u, col, xt, t0, t1, ft, g):
+            n = t1 - t0
+            nc.vector.tensor_tensor(
+                out=u[:, PACK * col : PACK * (col + n)].rearrange("p (c i j) -> p c j i", i=2, j=PACK),
+                in0=xt[:, :, t0:t1].rearrange("p j (c i) -> p c j i", i=2),
+                in1=ft[:, g, 0:PACK].rearrange("p (a j b) -> p a j b", a=1, b=1).to_broadcast([P, n // 2, PACK, 2]),
+                op=ALU.mult,
+            )
+
+        def scale_on_scalar(stage, col, xt, t0, t1, ft, g):
+            for j in range(PACK):
+                nc.scalar.activation(
+                    out=stage[:, j, col : col + t1 - t0], in_=xt[:, j, t0:t1], func=ACT.Copy, scale=ft[:, g, j : j + 1]
+                )
+
+        def interleave_on_scalar(u, col, stage, c0, c1):
+            nc.scalar.copy(
+                out=u[:, PACK * col : PACK * (col + c1 - c0)].rearrange("p (c i j) -> p c j i", i=4, j=PACK),
+                in_=stage[:, :, c0:c1].rearrange("p j (c i) -> p c j i", i=4),
+            )
+
+        def quantize(name, u, fmt):
+            width = u.shape[1] // PACK
+            codes = sb.tile([P, width], U32, name=name + "_codes", align_bytes=64)
+            plane = sb.tile([P, width], U8, name=name + "_plane", align_bytes=64)
+            nc.vector.quantize_mx(out=codes[:].bitcast(fmt), scales=plane[:], in_=u[:])
+            return codes, plane
+
+        acc = [ps.tile([P, T], F32, name="acc%d" % m) for m in range(M_TILES)]
+
+        def multiply(wt, wfmt, wplane, g, q, ufmt, col, n, start=False, stop=False):
+            codes, plane = q
+            wb_col = wt.shape[2] // N
+            for c in range(0, codes.shape[1], n):
+                for m in range(M_TILES):
+                    nc.tensor.matmul_mx(
+                        out=acc[m][:, col + c : col + c + n],
+                        lhsT=wt[:, g, m * P * wb_col : (m + 1) * P * wb_col].bitcast(wfmt),
+                        lhsT_scale=wplane[:, g, m * P : (m + 1) * P],
+                        rhs=codes[:, c : c + n].bitcast(ufmt),
+                        rhs_scale=plane[:, c : c + n],
+                        start=start,
+                        stop=stop,
+                    )
+
+        x0 = [load_x(0, 0, 128)]
+        fa_t = load_factor("fa_t", fa)
+        fb_t = load_factor("fb_t", fb)
+        fd_t = load_factor("fd_t", fd)
+        x0.append(load_x(0, 128, 256))
+        x0.append(load_x(0, 256, 512))
+        zeros = sb.tile([P, 8], F32, name="zeros")
+        nc.vector.memset(zeros[:], 0.0)
+        sa = new_plane("sa")
+        sc = new_plane("sc")
+        sbp = new_plane("sbp")
+        wa = load_words("wa", wa_words)
+        x1 = load_x(1, 0, T)
+        load_plane(nc.sync, sa, wa_scales)
+        wb = load_words("wb", wb_words.rearrange("g p n t -> g p (n t)"))
+        wc = load_words("wc", wc_words)
+        load_plane(nc.sync, sbp, wb_scales)
+        load_plane(nc.sync, sc, wc_scales)
+
+        ua0 = new_u("ua0", T, 0)
+        ua1 = [new_u("ua1_%d" % i, 128, 0) for i in range(4)]
+        ub = [new_u("ub%d" % g, T, 0) for g in range(PASSES)]
+        uc0 = new_u("uc0", T, 2)
+        uc1 = [new_u("uc1_%d" % i, 128, 2 if i == 0 else 0) for i in range(4)]
+        stage_b = [sb.tile([P, PACK, T], BF16, name="stage_b%d" % g, align_bytes=64) for g in range(PASSES)]
+        stage_c = sb.tile([P, PACK, 256], BF16, name="stage_c", align_bytes=64)
+
+        for g in range(PASSES):
+            nc.scalar.activation(
+                out=stage_b[g][:, :, 0:1], in_=zeros[:, 0:PACK].rearrange("p (j o) -> p j o", o=1), func=ACT.Copy
+            )
+        for xt, (t0, t1) in zip(x0, X0_CHUNKS):
+            scale_on_scalar(stage_b[0], t0 + 1, xt, 0, min(t1, T - 1) - t0, fb_t, 0)
+        interleave_on_scalar(ub[0], 0, stage_b[0], 0, 256)
+        interleave_on_scalar(ub[0], 256, stage_b[0], 256, T)
+        scale_on_scalar(stage_b[1], 1, x1, 0, 255, fb_t, 1)
+        scale_on_scalar(stage_b[1], 256, x1, 255, T - 1, fb_t, 1)
+        interleave_on_scalar(ub[1], 0, stage_b[1], 0, 256)
+        interleave_on_scalar(ub[1], 256, stage_b[1], 256, T)
+        scale_on_scalar(stage_c, 0, x1, 254, 382, fd_t, 1)
+        scale_on_scalar(stage_c, 128, x1, 382, 510, fd_t, 1)
+        interleave_on_scalar(uc1[2], 0, stage_c, 0, 128)
+        interleave_on_scalar(uc1[3], 0, stage_c, 128, 256)
+
+        def mul_a1(i):
+            multiply(wa, E2M1, sa, 1, quantize("a1_%d" % i, ua1[i], E4M3), E4M3, 128 * i, 128)
+
+        def mul_c1(i, stop=False):
+            multiply(wc, E2M1, sc, 1, quantize("c1_%d" % i, uc1[i], E4M3), E4M3, 128 * i, 128, stop=stop)
+
+        scale_on_vector(ua0, 0, x0[0], 0, 128, fa_t, 0)
+        scale_on_vector(ua0, 128, x0[1], 0, 128, fa_t, 0)
+        scale_on_vector(ua0, 256, x0[2], 0, 256, fa_t, 0)
+        scale_on_vector(uc0, 2, x0[0], 0, 128, fd_t, 0)
+        multiply(wa, E2M1, sa, 0, quantize("a0", ua0, E4M3), E4M3, 0, T, start=True)
+        scale_on_vector(uc0, 130, x0[1], 0, 128, fd_t, 0)
+        scale_on_vector(uc0, 258, x0[2], 0, 254, fd_t, 0)
+        multiply(wb, E4M3, sbp, 0, quantize("b0", ub[0], E5M2), E5M2, 0, T)
+        multiply(wc, E2M1, sc, 0, quantize("c0", uc0, E4M3), E4M3, 0, T)
+        scale_on_vector(ua1[0], 0, x1, 0, 128, fa_t, 1)
+        scale_on_vector(ua1[1], 0, x1, 128, 256, fa_t, 1)
+        mul_a1(0)
+        scale_on_vector(ua1[2], 0, x1, 256, 384, fa_t, 1)
+        mul_a1(1)
+        scale_on_vector(ua1[3], 0, x1, 384, 512, fa_t, 1)
+        mul_a1(2)
+        multiply(wb, E4M3, sbp, 1, quantize("b1", ub[1], E5M2), E5M2, 0, T)
+        mul_a1(3)
+        scale_on_vector(uc1[0], 2, x1, 0, 126, fd_t, 1)
+        scale_on_vector(uc1[1], 0, x1, 126, 254, fd_t, 1)
+        mul_c1(0)
+        mul_c1(2)
+        mul_c1(1)
+        mul_c1(3, stop=True)
+
+        for m in range(M_TILES):
+            res = sb.tile([P, T], F32, name="res%d" % m)
+            if m % 2 == 0:
+                nc.vector.tensor_scalar(out=res[:], in0=acc[m][:], scalar1=0.0, scalar2=None, op0=ALU.max)
+            else:
+                nc.scalar.activation(out=res[:], in_=acc[m][:], func=ACT.Relu)
+            nc.sync.dma_start(out=out[m * P : (m + 1) * P, :], in_=res[:])

@@ -20,7 +20,7 @@ P = 128
 PACK = 4
 PASSES = K // (P * PACK)
 M_TILES = N // P
-X0_CHUNKS = ((0, 128), (128, 256), (256, 512))
+B1_SCALAR = 192
 
 
 def tile_mix_three_windows_one_sum_kernel(
@@ -44,10 +44,10 @@ def tile_mix_three_windows_one_sum_kernel(
             nc.sync.dma_start(out=ft[:, :, 0:PACK], in_=f.rearrange("(g p j) o -> p g (j o)", g=PASSES, j=PACK))
             return ft
 
-        def load_words(name, words):
-            wt = sb.tile([P, PASSES, words.shape[2]], U8, name=name, align_bytes=64)
-            nc.sync.dma_start(out=wt[:].bitcast(I32), in_=words.rearrange("g p b -> p g b").bitcast(I32))
-            return wt
+        def load_words(name, words, g0, g1):
+            wt = sb.tile([P, g1 - g0, words.shape[2]], U8, name=name, align_bytes=64)
+            nc.sync.dma_start(out=wt[:].bitcast(I32), in_=words[g0:g1].rearrange("g p b -> p g b").bitcast(I32))
+            return [wt[:, g, :] for g in range(g1 - g0)]
 
         def new_plane(name):
             plane = sb.tile([P, PASSES, N], U8, name=name, align_bytes=64)
@@ -90,25 +90,28 @@ def tile_mix_three_windows_one_sum_kernel(
             width = u.shape[1] // PACK
             codes = sb.tile([P, width], U32, name=name + "_codes", align_bytes=64)
             plane = sb.tile([P, width], U8, name=name + "_plane", align_bytes=64)
-            nc.vector.quantize_mx(out=codes[:].bitcast(fmt), scales=plane[:], in_=u[:])
+            nc.vector.quantize_mx(out=codes[:].bitcast(fmt), scales=plane[:], in_=u)
             return codes, plane
 
         acc = [ps.tile([P, T], F32, name="acc%d" % m) for m in range(M_TILES)]
 
-        def multiply(wt, wfmt, wplane, g, q, ufmt, col, n, start=False, stop=False):
+        def one_pass(m, w, wfmt, wplane, q, ufmt, c, col, n, start=False, stop=False):
             codes, plane = q
-            wb_col = wt.shape[2] // N
-            for c in range(0, codes.shape[1], n):
+            step = w.shape[1] // M_TILES
+            nc.tensor.matmul_mx(
+                out=acc[m][:, col : col + n],
+                lhsT=w[:, m * step : (m + 1) * step].bitcast(wfmt),
+                lhsT_scale=wplane[:, m * P : (m + 1) * P],
+                rhs=codes[:, c : c + n].bitcast(ufmt),
+                rhs_scale=plane[:, c : c + n],
+                start=start,
+                stop=stop,
+            )
+
+        def multiply(w, wfmt, wplane, q, ufmt, col, n, start=False):
+            for c in range(0, q[0].shape[1], n):
                 for m in range(M_TILES):
-                    nc.tensor.matmul_mx(
-                        out=acc[m][:, col + c : col + c + n],
-                        lhsT=wt[:, g, m * P * wb_col : (m + 1) * P * wb_col].bitcast(wfmt),
-                        lhsT_scale=wplane[:, g, m * P : (m + 1) * P],
-                        rhs=codes[:, c : c + n].bitcast(ufmt),
-                        rhs_scale=plane[:, c : c + n],
-                        start=start,
-                        stop=stop,
-                    )
+                    one_pass(m, w, wfmt, wplane, q, ufmt, c, col + c, n, start=start and c == 0)
 
         x0 = [load_x(0, 0, 128)]
         fa_t = load_factor("fa_t", fa)
@@ -121,69 +124,69 @@ def tile_mix_three_windows_one_sum_kernel(
         sa = new_plane("sa")
         sc = new_plane("sc")
         sbp = new_plane("sbp")
-        wa = load_words("wa", wa_words)
-        x1 = load_x(1, 0, T)
+        wa = load_words("wa0", wa_words, 0, 1)
         load_plane(nc.sync, sa, wa_scales)
-        wb = load_words("wb", wb_words.rearrange("g p n t -> g p (n t)"))
-        wc = load_words("wc", wc_words)
-        load_plane(nc.sync, sbp, wb_scales)
+        x1 = load_x(1, 0, T)
         load_plane(nc.sync, sc, wc_scales)
+        wc = load_words("wc", wc_words, 0, 2)
+        wb = load_words("wb", wb_words.rearrange("g p n t -> g p (n t)"), 0, 2)
+        wa = wa + load_words("wa1", wa_words, 1, 2)
+        load_plane(nc.sync, sbp, wb_scales)
 
-        ua0 = new_u("ua0", T, 0)
+        ua0 = [new_u("ua0_%d" % i, 256, 0) for i in range(2)]
         ua1 = [new_u("ua1_%d" % i, 128, 0) for i in range(4)]
-        ub = [new_u("ub%d" % g, T, 0) for g in range(PASSES)]
+        ub0 = new_u("ub0", T, 0)
+        ub1 = new_u("ub1", T + 4, 1)
         uc0 = new_u("uc0", T, 2)
-        uc1 = [new_u("uc1_%d" % i, 128, 2 if i == 0 else 0) for i in range(4)]
-        stage_b = [sb.tile([P, PACK, T], BF16, name="stage_b%d" % g, align_bytes=64) for g in range(PASSES)]
-        stage_c = sb.tile([P, PACK, 256], BF16, name="stage_c", align_bytes=64)
+        uc1 = [new_u("uc1_%d" % i, 128, 0) for i in range(4)]
+        stage_b0 = sb.tile([P, PACK, T], BF16, name="stage_b0", align_bytes=64)
+        stage_b1 = sb.tile([P, PACK, B1_SCALAR], BF16, name="stage_b1", align_bytes=64)
+        stage_c = [sb.tile([P, PACK, 128], BF16, name="stage_c%d" % i, align_bytes=64) for i in range(4)]
 
-        for g in range(PASSES):
-            nc.scalar.activation(
-                out=stage_b[g][:, :, 0:1], in_=zeros[:, 0:PACK].rearrange("p (j o) -> p j o", o=1), func=ACT.Copy
-            )
-        for xt, (t0, t1) in zip(x0, X0_CHUNKS):
-            scale_on_scalar(stage_b[0], t0 + 1, xt, 0, min(t1, T - 1) - t0, fb_t, 0)
-        interleave_on_scalar(ub[0], 0, stage_b[0], 0, 256)
-        interleave_on_scalar(ub[0], 256, stage_b[0], 256, T)
-        scale_on_scalar(stage_b[1], 1, x1, 0, 255, fb_t, 1)
-        scale_on_scalar(stage_b[1], 256, x1, 255, T - 1, fb_t, 1)
-        interleave_on_scalar(ub[1], 0, stage_b[1], 0, 256)
-        interleave_on_scalar(ub[1], 256, stage_b[1], 256, T)
-        scale_on_scalar(stage_c, 0, x1, 254, 382, fd_t, 1)
-        scale_on_scalar(stage_c, 128, x1, 382, 510, fd_t, 1)
-        interleave_on_scalar(uc1[2], 0, stage_c, 0, 128)
-        interleave_on_scalar(uc1[3], 0, stage_c, 128, 256)
+        nc.scalar.activation(
+            out=stage_b0[:, :, 0:1], in_=zeros[:, 0:PACK].rearrange("p (j o) -> p j o", o=1), func=ACT.Copy
+        )
+        nc.scalar.activation(
+            out=stage_c[0][:, :, 0:2], in_=zeros[:].rearrange("p (j o) -> p j o", o=2), func=ACT.Copy
+        )
+        scale_on_scalar(stage_b0, 1, x0[0], 0, 128, fb_t, 0)
+        scale_on_scalar(stage_b0, 129, x0[1], 0, 128, fb_t, 0)
+        interleave_on_scalar(ub0, 0, stage_b0, 0, 128)
+        scale_on_scalar(stage_b0, 257, x0[2], 0, 255, fb_t, 0)
+        interleave_on_scalar(ub0, 128, stage_b0, 128, 256)
+        interleave_on_scalar(ub0, 256, stage_b0, 256, T)
+        scale_on_scalar(stage_b1, 0, x1, 0, B1_SCALAR, fb_t, 1)
+        scale_on_scalar(stage_c[0], 2, x1, 0, 126, fd_t, 1)
+        interleave_on_scalar(ub1, 1, stage_b1, 0, B1_SCALAR)
+        for i in range(4):
+            if i + 1 < 4:
+                scale_on_scalar(stage_c[i + 1], 0, x1, 128 * i + 126, 128 * i + 254, fd_t, 1)
+            interleave_on_scalar(uc1[i], 0, stage_c[i], 0, 128)
 
-        def mul_a1(i):
-            multiply(wa, E2M1, sa, 1, quantize("a1_%d" % i, ua1[i], E4M3), E4M3, 128 * i, 128)
-
-        def mul_c1(i, stop=False):
-            multiply(wc, E2M1, sc, 1, quantize("c1_%d" % i, uc1[i], E4M3), E4M3, 128 * i, 128, stop=stop)
-
-        scale_on_vector(ua0, 0, x0[0], 0, 128, fa_t, 0)
-        scale_on_vector(ua0, 128, x0[1], 0, 128, fa_t, 0)
-        scale_on_vector(ua0, 256, x0[2], 0, 256, fa_t, 0)
+        scale_on_vector(ua0[0], 0, x0[0], 0, 128, fa_t, 0)
         scale_on_vector(uc0, 2, x0[0], 0, 128, fd_t, 0)
-        multiply(wa, E2M1, sa, 0, quantize("a0", ua0, E4M3), E4M3, 0, T, start=True)
+        scale_on_vector(ua0[0], 128, x0[1], 0, 128, fa_t, 0)
         scale_on_vector(uc0, 130, x0[1], 0, 128, fd_t, 0)
+        multiply(wa[0], E2M1, sa[:, 0, :], quantize("a0_0", ua0[0][:], E4M3), E4M3, 0, 128, start=True)
+        scale_on_vector(ua0[1], 0, x0[2], 0, 256, fa_t, 0)
         scale_on_vector(uc0, 258, x0[2], 0, 254, fd_t, 0)
-        multiply(wb, E4M3, sbp, 0, quantize("b0", ub[0], E5M2), E5M2, 0, T)
-        multiply(wc, E2M1, sc, 0, quantize("c0", uc0, E4M3), E4M3, 0, T)
+        multiply(wa[0], E2M1, sa[:, 0, :], quantize("a0_1", ua0[1][:], E4M3), E4M3, 256, 128)
+        multiply(wc[0], E2M1, sc[:, 0, :], quantize("c0", uc0[:], E4M3), E4M3, 0, T)
+        scale_on_vector(ub1, B1_SCALAR + 1, x1, B1_SCALAR, T, fb_t, 1)
+        multiply(wb[0], E4M3, sbp[:, 0, :], quantize("b0", ub0[:], E5M2), E5M2, 0, T)
         scale_on_vector(ua1[0], 0, x1, 0, 128, fa_t, 1)
-        scale_on_vector(ua1[1], 0, x1, 128, 256, fa_t, 1)
-        mul_a1(0)
-        scale_on_vector(ua1[2], 0, x1, 256, 384, fa_t, 1)
-        mul_a1(1)
-        scale_on_vector(ua1[3], 0, x1, 384, 512, fa_t, 1)
-        mul_a1(2)
-        multiply(wb, E4M3, sbp, 1, quantize("b1", ub[1], E5M2), E5M2, 0, T)
-        mul_a1(3)
-        scale_on_vector(uc1[0], 2, x1, 0, 126, fd_t, 1)
-        scale_on_vector(uc1[1], 0, x1, 126, 254, fd_t, 1)
-        mul_c1(0)
-        mul_c1(2)
-        mul_c1(1)
-        mul_c1(3, stop=True)
+        multiply(wb[1], E4M3, sbp[:, 1, :], quantize("b1", ub1[:, 0 : PACK * T], E5M2), E5M2, 0, T)
+        for i in range(3):
+            scale_on_vector(ua1[i + 1], 0, x1, 128 * (i + 1), 128 * (i + 2), fa_t, 1)
+            qa = quantize("a1_%d" % i, ua1[i][:], E4M3)
+            multiply(wa[1], E2M1, sa[:, 1, :], qa, E4M3, 128 * i, 128)
+            qc = quantize("c1_%d" % i, uc1[i][:], E4M3)
+            multiply(wc[1], E2M1, sc[:, 1, :], qc, E4M3, 128 * i, 128)
+        qa = quantize("a1_3", ua1[3][:], E4M3)
+        qc = quantize("c1_3", uc1[3][:], E4M3)
+        for m in range(M_TILES):
+            one_pass(m, wa[1], E2M1, sa[:, 1, :], qa, E4M3, 0, 384, 128)
+            one_pass(m, wc[1], E2M1, sc[:, 1, :], qc, E4M3, 0, 384, 128, stop=True)
 
         for m in range(M_TILES):
             res = sb.tile([P, T], F32, name="res%d" % m)

@@ -124,16 +124,19 @@ def tile_mix_three_windows_one_sum_kernel(
         sa = new_plane("sa")
         sc = new_plane("sc")
         sbp = new_plane("sbp")
+        x1 = load_x(1, 0, 256)
         wa = load_words("wa0", wa_words, 0, 1)
         load_plane(nc.sync, sa, wa_scales)
-        x1 = load_x(1, 0, T)
-        load_plane(nc.sync, sc, wc_scales)
-        wc = load_words("wc", wc_words, 0, 2)
-        wb = load_words("wb", wb_words.rearrange("g p n t -> g p (n t)"), 0, 2)
-        wa = wa + load_words("wa1", wa_words, 1, 2)
+        x1r = load_x(1, 248, T)
         load_plane(nc.sync, sbp, wb_scales)
+        wb_rows = wb_words.rearrange("g p n t -> g p (n t)")
+        wb = load_words("wb0", wb_rows, 0, 1)
+        wc = load_words("wc", wc_words, 0, 2)
+        load_plane(nc.sync, sc, wc_scales)
+        wb = wb + load_words("wb1", wb_rows, 1, 2)
+        wa = wa + load_words("wa1", wa_words, 1, 2)
 
-        ua0 = [new_u("ua0_%d" % i, 256, 0) for i in range(2)]
+        ua0 = new_u("ua0", T, 0)
         ua1 = [new_u("ua1_%d" % i, 128, 0) for i in range(4)]
         ub0 = new_u("ub0", T, 0)
         ub1 = new_u("ub1", T + 4, 1)
@@ -160,38 +163,43 @@ def tile_mix_three_windows_one_sum_kernel(
         interleave_on_scalar(ub1, 1, stage_b1, 0, B1_SCALAR)
         for i in range(4):
             if i + 1 < 4:
-                scale_on_scalar(stage_c[i + 1], 0, x1, 128 * i + 126, 128 * i + 254, fd_t, 1)
+                xt, first = (x1, 0) if i == 0 else (x1r, 248)
+                scale_on_scalar(stage_c[i + 1], 0, xt, 128 * i + 126 - first, 128 * i + 254 - first, fd_t, 1)
             interleave_on_scalar(uc1[i], 0, stage_c[i], 0, 128)
 
-        scale_on_vector(ua0[0], 0, x0[0], 0, 128, fa_t, 0)
+        scale_on_vector(ua0, 0, x0[0], 0, 128, fa_t, 0)
         scale_on_vector(uc0, 2, x0[0], 0, 128, fd_t, 0)
-        scale_on_vector(ua0[0], 128, x0[1], 0, 128, fa_t, 0)
+        scale_on_vector(ua0, 128, x0[1], 0, 128, fa_t, 0)
+        scale_on_vector(ua0, 256, x0[2], 0, 256, fa_t, 0)
         scale_on_vector(uc0, 130, x0[1], 0, 128, fd_t, 0)
-        multiply(wa[0], E2M1, sa[:, 0, :], quantize("a0_0", ua0[0][:], E4M3), E4M3, 0, 128, start=True)
-        scale_on_vector(ua0[1], 0, x0[2], 0, 256, fa_t, 0)
+        multiply(wa[0], E2M1, sa[:, 0, :], quantize("a0", ua0[:], E4M3), E4M3, 0, T, start=True)
         scale_on_vector(uc0, 258, x0[2], 0, 254, fd_t, 0)
-        multiply(wa[0], E2M1, sa[:, 0, :], quantize("a0_1", ua0[1][:], E4M3), E4M3, 256, 128)
-        multiply(wc[0], E2M1, sc[:, 0, :], quantize("c0", uc0[:], E4M3), E4M3, 0, T)
-        scale_on_vector(ub1, B1_SCALAR + 1, x1, B1_SCALAR, T, fb_t, 1)
         multiply(wb[0], E4M3, sbp[:, 0, :], quantize("b0", ub0[:], E5M2), E5M2, 0, T)
+        multiply(wc[0], E2M1, sc[:, 0, :], quantize("c0", uc0[:], E4M3), E4M3, 0, T)
+        scale_on_vector(ub1, B1_SCALAR + 1, x1, B1_SCALAR, 256, fb_t, 1)
+        scale_on_vector(ub1, 257, x1r, 8, 264, fb_t, 1)
         scale_on_vector(ua1[0], 0, x1, 0, 128, fa_t, 1)
         multiply(wb[1], E4M3, sbp[:, 1, :], quantize("b1", ub1[:, 0 : PACK * T], E5M2), E5M2, 0, T)
-        for i in range(3):
-            scale_on_vector(ua1[i + 1], 0, x1, 128 * (i + 1), 128 * (i + 2), fa_t, 1)
-            qa = quantize("a1_%d" % i, ua1[i][:], E4M3)
-            multiply(wa[1], E2M1, sa[:, 1, :], qa, E4M3, 128 * i, 128)
-            qc = quantize("c1_%d" % i, uc1[i][:], E4M3)
-            multiply(wc[1], E2M1, sc[:, 1, :], qc, E4M3, 128 * i, 128)
-        qa = quantize("a1_3", ua1[3][:], E4M3)
-        qc = quantize("c1_3", uc1[3][:], E4M3)
+        qa = []
+        qc = []
+        for i in range(4):
+            if i + 1 < 4:
+                xt, first = (x1, 0) if i == 0 else (x1r, 248)
+                scale_on_vector(ua1[i + 1], 0, xt, 128 * (i + 1) - first, 128 * (i + 2) - first, fa_t, 1)
+            qa.append(quantize("a1_%d" % i, ua1[i][:], E4M3))
+            qc.append(quantize("c1_%d" % i, uc1[i][:], E4M3))
+            if i < 2:
+                multiply(wa[1], E2M1, sa[:, 1, :], qa[i], E4M3, 128 * i, 128)
+                multiply(wc[1], E2M1, sc[:, 1, :], qc[i], E4M3, 128 * i, 128)
         for m in range(M_TILES):
-            one_pass(m, wa[1], E2M1, sa[:, 1, :], qa, E4M3, 0, 384, 128)
-            one_pass(m, wc[1], E2M1, sc[:, 1, :], qc, E4M3, 0, 384, 128, stop=True)
+            for i in range(2, 4):
+                one_pass(m, wa[1], E2M1, sa[:, 1, :], qa[i], E4M3, 0, 128 * i, 128)
+                one_pass(m, wc[1], E2M1, sc[:, 1, :], qc[i], E4M3, 0, 128 * i, 128, stop=(i == 3))
 
-        for m in range(M_TILES):
-            res = sb.tile([P, T], F32, name="res%d" % m)
+        for m, c0, c1 in ((0, 0, 256), (1, 0, 256), (0, 256, T), (1, 256, T), (2, 0, T), (3, 0, T)):
+            res = sb.tile([P, c1 - c0], F32, name="res%d_%d" % (m, c0))
             if m % 2 == 0:
-                nc.vector.tensor_scalar(out=res[:], in0=acc[m][:], scalar1=0.0, scalar2=None, op0=ALU.max)
+                nc.vector.tensor_scalar(out=res[:], in0=acc[m][:, c0:c1], scalar1=0.0, scalar2=None, op0=ALU.max)
             else:
-                nc.scalar.activation(out=res[:], in_=acc[m][:], func=ACT.Relu)
-            nc.sync.dma_start(out=out[m * P : (m + 1) * P, :], in_=res[:])
+                nc.scalar.activation(out=res[:], in_=acc[m][:, c0:c1], func=ACT.Relu)
+            nc.sync.dma_start(out=out[m * P : (m + 1) * P, c0:c1], in_=res[:])

from contextlib import ExitStack

import concourse.mybir as mybir

K, T, N = 1024, 512, 512
FLOPS = 3 * 2 * K * T * N

F32 = mybir.dt.float32
BF16 = mybir.dt.bfloat16
I32 = mybir.dt.int32
U32 = mybir.dt.uint32
U8 = mybir.dt.uint8
E4M3 = mybir.dt.float8_e4m3fn_x4
E5M2 = mybir.dt.float8_e5m2_x4
E2M1 = mybir.dt.float4_e2m1fn_x4
ALU = mybir.AluOpType
ACT = mybir.ActivationFunctionType

P = 128
PACK = 4
PASSES = K // (P * PACK)
M_TILES = N // P
B1_SCALAR = 192


def tile_mix_three_windows_one_sum_kernel(
    tc, xf, fa, fb, fd, wa_words, wa_scales, wb_words, wb_scales, wc_words, wc_scales, out
):
    nc = tc.nc
    with ExitStack() as ctx:
        sb = ctx.enter_context(tc.tile_pool(name="sb", bufs=1))
        ps = ctx.enter_context(tc.psum_pool(name="ps", bufs=1))
        ctx.enter_context(tc.manual_schedule())

        x_rows = xf.rearrange("(g p j) t -> g p j t", g=PASSES, j=PACK)

        def load_x(g, t0, t1):
            xt = sb.tile([P, PACK, t1 - t0], F32, name="x_%d_%d" % (g, t0), align_bytes=64)
            nc.sync.dma_start(out=xt[:], in_=x_rows[g, :, :, t0:t1])
            return xt

        def load_factor(name, f):
            ft = sb.tile([P, PASSES, 8], F32, name=name)
            nc.sync.dma_start(out=ft[:, :, 0:PACK], in_=f.rearrange("(g p j) o -> p g (j o)", g=PASSES, j=PACK))
            return ft

        def load_words(name, words, g0, g1):
            wt = sb.tile([P, g1 - g0, words.shape[2]], U8, name=name, align_bytes=64)
            nc.sync.dma_start(out=wt[:].bitcast(I32), in_=words[g0:g1].rearrange("g p b -> p g b").bitcast(I32))
            return [wt[:, g, :] for g in range(g1 - g0)]

        def new_plane(name):
            plane = sb.tile([P, PASSES, N], U8, name=name, align_bytes=64)
            nc.vector.memset(plane[:].bitcast(I32), 0)
            return plane

        def load_plane(queue, plane, scales):
            rows = scales.rearrange("g (q r) n -> r q g n", r=4)
            for r in range(4):
                queue.dma_start(out=plane[r:P:32].bitcast(I32), in_=rows[r].bitcast(I32))

        def new_u(name, width, pad):
            u = sb.tile([P, PACK * width], BF16, name=name, align_bytes=64)
            if pad:
                nc.vector.memset(u[:, 0 : PACK * pad], 0.0)
            return u

        def scale_on_vector(u, col, xt, t0, t1, ft, g):
            n = t1 - t0
            nc.vector.tensor_tensor(
                out=u[:, PACK * col : PACK * (col + n)].rearrange("p (c i j) -> p c j i", i=2, j=PACK),
                in0=xt[:, :, t0:t1].rearrange("p j (c i) -> p c j i", i=2),
                in1=ft[:, g, 0:PACK].rearrange("p (a j b) -> p a j b", a=1, b=1).to_broadcast([P, n // 2, PACK, 2]),
                op=ALU.mult,
            )

        def scale_on_scalar(stage, col, xt, t0, t1, ft, g):
            for j in range(PACK):
                nc.scalar.activation(
                    out=stage[:, j, col : col + t1 - t0], in_=xt[:, j, t0:t1], func=ACT.Copy, scale=ft[:, g, j : j + 1]
                )

        def interleave_on_scalar(u, col, stage, c0, c1):
            nc.scalar.copy(
                out=u[:, PACK * col : PACK * (col + c1 - c0)].rearrange("p (c i j) -> p c j i", i=4, j=PACK),
                in_=stage[:, :, c0:c1].rearrange("p j (c i) -> p c j i", i=4),
            )

        def quantize(name, u, fmt):
            width = u.shape[1] // PACK
            codes = sb.tile([P, width], U32, name=name + "_codes", align_bytes=64)
            plane = sb.tile([P, width], U8, name=name + "_plane", align_bytes=64)
            nc.vector.quantize_mx(out=codes[:].bitcast(fmt), scales=plane[:], in_=u)
            return codes, plane

        acc = [ps.tile([P, T], F32, name="acc%d" % m) for m in range(M_TILES)]

        def one_pass(m, w, wfmt, wplane, q, ufmt, c, col, n, start=False, stop=False):
            codes, plane = q
            step = w.shape[1] // M_TILES
            nc.tensor.matmul_mx(
                out=acc[m][:, col : col + n],
                lhsT=w[:, m * step : (m + 1) * step].bitcast(wfmt),
                lhsT_scale=wplane[:, m * P : (m + 1) * P],
                rhs=codes[:, c : c + n].bitcast(ufmt),
                rhs_scale=plane[:, c : c + n],
                start=start,
                stop=stop,
            )

        def multiply(w, wfmt, wplane, q, ufmt, col, n, start=False):
            for c in range(0, q[0].shape[1], n):
                for m in range(M_TILES):
                    one_pass(m, w, wfmt, wplane, q, ufmt, c, col + c, n, start=start and c == 0)

        x0 = [load_x(0, 0, 128)]
        fa_t = load_factor("fa_t", fa)
        fb_t = load_factor("fb_t", fb)
        fd_t = load_factor("fd_t", fd)
        x0.append(load_x(0, 128, 256))
        x0.append(load_x(0, 256, 512))
        zeros = sb.tile([P, 8], F32, name="zeros")
        nc.vector.memset(zeros[:], 0.0)
        sa = new_plane("sa")
        sc = new_plane("sc")
        sbp = new_plane("sbp")
        x1 = load_x(1, 0, 256)
        wa = load_words("wa0", wa_words, 0, 1)
        load_plane(nc.sync, sa, wa_scales)
        x1r = load_x(1, 248, T)
        load_plane(nc.sync, sbp, wb_scales)
        wb_rows = wb_words.rearrange("g p n t -> g p (n t)")
        wb = load_words("wb0", wb_rows, 0, 1)
        wc = load_words("wc", wc_words, 0, 2)
        load_plane(nc.sync, sc, wc_scales)
        wb = wb + load_words("wb1", wb_rows, 1, 2)
        wa = wa + load_words("wa1", wa_words, 1, 2)

        ua0 = new_u("ua0", T, 0)
        ua1 = [new_u("ua1_%d" % i, 128, 0) for i in range(4)]
        ub0 = new_u("ub0", T, 0)
        ub1 = new_u("ub1", T + 4, 1)
        uc0 = new_u("uc0", T, 2)
        uc1 = [new_u("uc1_%d" % i, 128, 0) for i in range(4)]
        stage_b0 = sb.tile([P, PACK, T], BF16, name="stage_b0", align_bytes=64)
        stage_b1 = sb.tile([P, PACK, B1_SCALAR], BF16, name="stage_b1", align_bytes=64)
        stage_c = [sb.tile([P, PACK, 128], BF16, name="stage_c%d" % i, align_bytes=64) for i in range(4)]

        nc.scalar.activation(
            out=stage_b0[:, :, 0:1], in_=zeros[:, 0:PACK].rearrange("p (j o) -> p j o", o=1), func=ACT.Copy
        )
        nc.scalar.activation(
            out=stage_c[0][:, :, 0:2], in_=zeros[:].rearrange("p (j o) -> p j o", o=2), func=ACT.Copy
        )
        scale_on_scalar(stage_b0, 1, x0[0], 0, 128, fb_t, 0)
        scale_on_scalar(stage_b0, 129, x0[1], 0, 128, fb_t, 0)
        interleave_on_scalar(ub0, 0, stage_b0, 0, 128)
        scale_on_scalar(stage_b0, 257, x0[2], 0, 255, fb_t, 0)
        interleave_on_scalar(ub0, 128, stage_b0, 128, 256)
        interleave_on_scalar(ub0, 256, stage_b0, 256, T)
        scale_on_scalar(stage_b1, 0, x1, 0, B1_SCALAR, fb_t, 1)
        scale_on_scalar(stage_c[0], 2, x1, 0, 126, fd_t, 1)
        interleave_on_scalar(ub1, 1, stage_b1, 0, B1_SCALAR)
        for i in range(4):
            if i + 1 < 4:
                xt, first = (x1, 0) if i == 0 else (x1r, 248)
                scale_on_scalar(stage_c[i + 1], 0, xt, 128 * i + 126 - first, 128 * i + 254 - first, fd_t, 1)
            interleave_on_scalar(uc1[i], 0, stage_c[i], 0, 128)

        scale_on_vector(ua0, 0, x0[0], 0, 128, fa_t, 0)
        scale_on_vector(uc0, 2, x0[0], 0, 128, fd_t, 0)
        scale_on_vector(ua0, 128, x0[1], 0, 128, fa_t, 0)
        scale_on_vector(ua0, 256, x0[2], 0, 256, fa_t, 0)
        scale_on_vector(uc0, 130, x0[1], 0, 128, fd_t, 0)
        multiply(wa[0], E2M1, sa[:, 0, :], quantize("a0", ua0[:], E4M3), E4M3, 0, T, start=True)
        scale_on_vector(uc0, 258, x0[2], 0, 254, fd_t, 0)
        multiply(wb[0], E4M3, sbp[:, 0, :], quantize("b0", ub0[:], E5M2), E5M2, 0, T)
        multiply(wc[0], E2M1, sc[:, 0, :], quantize("c0", uc0[:], E4M3), E4M3, 0, T)
        scale_on_vector(ub1, B1_SCALAR + 1, x1, B1_SCALAR, 256, fb_t, 1)
        scale_on_vector(ub1, 257, x1r, 8, 264, fb_t, 1)
        scale_on_vector(ua1[0], 0, x1, 0, 128, fa_t, 1)
        multiply(wb[1], E4M3, sbp[:, 1, :], quantize("b1", ub1[:, 0 : PACK * T], E5M2), E5M2, 0, T)
        qa = []
        qc = []
        for i in range(4):
            if i + 1 < 4:
                xt, first = (x1, 0) if i == 0 else (x1r, 248)
                scale_on_vector(ua1[i + 1], 0, xt, 128 * (i + 1) - first, 128 * (i + 2) - first, fa_t, 1)
            qa.append(quantize("a1_%d" % i, ua1[i][:], E4M3))
            qc.append(quantize("c1_%d" % i, uc1[i][:], E4M3))
            if i < 2:
                multiply(wa[1], E2M1, sa[:, 1, :], qa[i], E4M3, 128 * i, 128)
                multiply(wc[1], E2M1, sc[:, 1, :], qc[i], E4M3, 128 * i, 128)
        for m in range(M_TILES):
            for i in range(2, 4):
                one_pass(m, wa[1], E2M1, sa[:, 1, :], qa[i], E4M3, 0, 128 * i, 128)
                one_pass(m, wc[1], E2M1, sc[:, 1, :], qc[i], E4M3, 0, 128 * i, 128, stop=(i == 3))

        for m, c0, c1 in ((0, 0, 256), (1, 0, 256), (0, 256, T), (1, 256, T), (2, 0, T), (3, 0, T)):
            res = sb.tile([P, c1 - c0], F32, name="res%d_%d" % (m, c0))
            if m % 2 == 0:
                nc.vector.tensor_scalar(out=res[:], in0=acc[m][:, c0:c1], scalar1=0.0, scalar2=None, op0=ALU.max)
            else:
                nc.scalar.activation(out=res[:], in_=acc[m][:, c0:c1], func=ACT.Relu)
            nc.sync.dma_start(out=out[m * P : (m + 1) * P, c0:c1], in_=res[:])
